import numpy as np
import ml_dtypes


def mxq(x, axis, fmt="e4m3"):
    dtype, down = {"e4m3": (ml_dtypes.float8_e4m3fn, 7), "e5m2": (ml_dtypes.float8_e5m2, 14)}[fmt]
    v = np.moveaxis(np.asarray(x, np.float32).astype(ml_dtypes.bfloat16).astype(np.float64), axis, -1)
    blocks = v.reshape(v.shape[:-1] + (-1, 32))
    amax = np.abs(blocks).max(-1, keepdims=True)
    byte = np.maximum(np.where(amax > 0, np.frexp(amax)[1] - 1 + 127, 0) - down, 1)
    scale = np.exp2(byte - 127.0)
    codes = (blocks / scale).astype(np.float32).astype(dtype).astype(np.float64)
    return np.moveaxis((codes * scale).reshape(v.shape), -1, axis)


WIDE = False


def mx_kscale(k):
    if not WIDE:
        return np.ones(k)
    levels = np.array([10, -10, 5, -5, 0])
    if k % 512:
        return np.exp2(np.random.permutation(np.resize(levels, k // 32))).repeat(32)
    a = np.empty((k // 512, 16))
    for p in range(k // 512):
        a[p, :8] = np.random.permutation(np.resize(levels, 8))
        for g in range(8):
            far = levels[np.abs(levels - a[p, g]) >= 10]
            a[p, g + 8] = far[np.random.randint(len(far))]
    return np.exp2(a.ravel()).repeat(32)


def f64(x):
    return np.asarray(x).astype(np.float64)


def striped(idx):
    return np.tile(idx.reshape(-1, 16).T, (8, 1)).astype(np.uint16)


def unstriped(offs):
    return offs[:16].T.reshape(-1).astype(np.int64)


K, T, S, H, N = 1024, 2048, 512, 512, 256


def setup_inputs():
    n = np.random.standard_normal
    s = mx_kscale(K)[:, None]
    u = mx_kscale(H)
    return {
        "xT": (n((K, T)) * s).astype(np.float32),
        "w1": (n((K, H)) / np.sqrt(K) / s).astype(np.float32),
        "w2": (n((H, N)) / np.sqrt(H) / u[:, None]).astype(np.float32),
        "gamma": (np.random.uniform(0.5, 1.5, (H, 1)) * u[:, None]).astype(np.float32),
        "offs": striped(np.random.permutation(T)[:S]),
    }


def reference(xT, w1, w2, gamma, offs):
    xq = mxq(f64(xT)[:, unstriped(offs)], 0, "e4m3")
    h = mxq(f64(w1), 0, "e4m3").T @ xq
    hn = (h - h.mean(axis=1, keepdims=True)) / np.sqrt(h.var(axis=1, keepdims=True) + 1e-5)
    z = f64(gamma) * hn
    return mxq(f64(w2), 0, "e4m3").T @ mxq(z, 0, "e4m3")

@@ -1,0 +1,162 @@
+from contextlib import ExitStack
+
+import concourse.mybir as mybir
+
+K, T, S, H, N = 1024, 2048, 512, 512, 256
+FLOPS = 2 * K * H * S + 2 * H * N * S
+EPS = 1e-5
+
+F32 = mybir.dt.float32
+BF16 = mybir.dt.bfloat16
+U32 = mybir.dt.uint32
+U16 = mybir.dt.uint16
+U8 = mybir.dt.uint8
+FP8X4 = mybir.dt.float8_e4m3fn_x4
+ALU = mybir.AluOpType
+ACT = mybir.ActivationFunctionType
+
+P = 128
+PACK = 4
+K_PASS = P * PACK
+HALF = S // 2
+W1_VECTOR_M = 88
+
+
+def tile_picked_inorm_none_e_kernel(tc, xT, w1, w2, gamma, offs, out):
+    nc = tc.nc
+    with ExitStack() as ctx:
+        sb = ctx.enter_context(tc.tile_pool(name="sb", bufs=1))
+        ps = ctx.enter_context(tc.psum_pool(name="ps", bufs=1))
+
+        def sbuf(name, shape, dtype):
+            return sb.tile(shape, dtype, name=name, align_bytes=64)
+
+        def quantize(codes, scales, values):
+            nc.vector.quantize_mx(out=codes.bitcast(FP8X4), scales=scales, in_=values)
+
+        def weave(engine_copy, dst, src):
+            engine_copy(
+                dst.rearrange("p (c i) j -> p c j i", i=4),
+                src.rearrange("p j (c i) -> p c j i", i=4),
+            )
+
+        x_rows = xT.rearrange("(g p j) t -> g j p t", p=P, j=PACK)
+        w1_rows = w1.rearrange("(g p j) c -> g p j c", p=P, j=PACK)
+        x_raw = [[sbuf("x_raw%d%d" % (g, j), [P, T], F32) for j in range(PACK)] for g in range(2)]
+        w1_raw = [sbuf("w1_raw%d" % g, [P, PACK, H], F32) for g in range(2)]
+        w2_raw = sbuf("w2_raw", [P, PACK, N], F32)
+        offsets = sb.tile([P, S // 16], U16, name="offsets")
+        gain = sbuf("gain", [P, PACK], F32)
+
+        nc.sync.dma_start(x_raw[0][0][:], x_rows[0, 0])
+        nc.sync.dma_start(offsets[:], offs)
+        nc.sync.dma_start(gain[:], gamma.rearrange("(p t) o -> p (t o)", t=PACK))
+        for j in range(1, PACK):
+            nc.sync.dma_start(x_raw[0][j][:], x_rows[0, j])
+        nc.sync.dma_start(w1_raw[0][:], w1_rows[0])
+        for j in range(PACK):
+            nc.sync.dma_start(x_raw[1][j][:], x_rows[1, j])
+        nc.sync.dma_start(w1_raw[1][:], w1_rows[1])
+        nc.sync.dma_start(w2_raw[:], w2.rearrange("(p j) n -> p j n", j=PACK))
+
+        one = sbuf("one", [P, 1], F32)
+        eps = sbuf("eps", [P, 1], F32)
+        nc.vector.memset(one[:], 1.0)
+        nc.scalar.activation(eps[:], one[:], ACT.Sqrt, scale=EPS * EPS)
+
+        h_banks = [ps.tile([P, S], F32, name="h%d" % t) for t in range(PACK)]
+        for g in range(2):
+            x_bf = sbuf("x_bf%d" % g, [P, S, PACK], BF16)
+            x_pair = sbuf("x_pair%d" % g, [P, 2, S], BF16)
+            for j in range(2):
+                nc.vector.tensor_copy(x_pair[:, j, :], x_raw[g][j][:].indirect(offsets[:]))
+            weave(nc.scalar.copy, x_bf[:, :, 0:2], x_pair[:])
+            for j in range(2, PACK):
+                nc.vector.tensor_copy(x_bf[:, :, j], x_raw[g][j][:].indirect(offsets[:]))
+            x_codes = sbuf("x_codes%d" % g, [P, S], U32)
+            x_scales = sbuf("x_scales%d" % g, [P, S], U8)
+            quantize(x_codes[:], x_scales[:], x_bf[:].rearrange("p n j -> p (n j)"))
+
+            w1_bf = sbuf("w1_bf%d" % g, [P, PACK, P, PACK], BF16)
+            dst = w1_bf[:].rearrange("p t m j -> p m j t")
+            src = w1_raw[g][:].rearrange("p j (m t) -> p m j t", t=PACK)
+            split = W1_VECTOR_M if g == 1 else 0
+            if split:
+                nc.vector.tensor_copy(dst[:, :split], src[:, :split])
+            nc.scalar.copy(dst[:, split:], src[:, split:])
+            for t in range(PACK):
+                w1_codes = sbuf("w1_codes%d%d" % (g, t), [P, P], U32)
+                w1_scales = sbuf("w1_scales%d%d" % (g, t), [P, P], U8)
+                quantize(w1_codes[:], w1_scales[:], w1_bf[:, t].rearrange("p m j -> p (m j)"))
+                nc.tensor.matmul_mx(
+                    out=h_banks[t][:],
+                    lhsT=w1_codes[:].bitcast(FP8X4),
+                    lhsT_scale=w1_scales[:],
+                    rhs=x_codes[:].bitcast(FP8X4),
+                    rhs_scale=x_scales[:],
+                    start=(g == 0),
+                    stop=(g == 1),
+                )
+
+        w2_bf = sbuf("w2_bf", [P, N, PACK], BF16)
+        weave(nc.scalar.copy, w2_bf[:], w2_raw[:])
+        w2_codes = sbuf("w2_codes", [P, N], U32)
+        w2_scales = sbuf("w2_scales", [P, N], U8)
+        quantize(w2_codes[:], w2_scales[:], w2_bf[:].rearrange("p n j -> p (n j)"))
+
+        z_rows = [sbuf("z_rows%d" % u, [P, PACK, HALF], BF16) for u in range(2)]
+        for pair in range(2):
+            ts = slice(2 * pair, 2 * pair + 2)
+            stats = sbuf("stats%d" % pair, [P, 2, 8], F32)
+            moments = sbuf("moments%d" % pair, [P, 2, 2], F32)
+            for e in range(2):
+                nc.vector.bn_stats(stats[:, e, 0:6], h_banks[2 * pair + e][:])
+            for e in range(2):
+                nc.vector.bn_aggr(moments[:, e, :], stats[:, e, 0:6])
+            std = sbuf("std%d" % pair, [P, 2], F32)
+            nc.scalar.activation(std[:], moments[:, :, 1], ACT.Sqrt, bias=eps[:])
+            rstd = sbuf("rstd%d" % pair, [P, 2], F32)
+            nc.vector.reciprocal(rstd[:], std[:])
+            factor = sbuf("factor%d" % pair, [P, 2], F32)
+            nc.vector.tensor_tensor(factor[:], rstd[:], gain[:, ts], ALU.mult)
+            shift = sbuf("shift%d" % pair, [P, 2], F32)
+            nc.vector.scalar_tensor_tensor(shift[:], moments[:, :, 0], -1.0, factor[:], ALU.mult, ALU.mult)
+            for u in range(2):
+                for e in range(2):
+                    t = 2 * pair + e
+                    src = h_banks[t][:, u * HALF : (u + 1) * HALF]
+                    if t == 2 and u == 0:
+                        nc.vector.tensor_scalar(
+                            z_rows[u][:, t, :], src, moments[:, e, 0:1], factor[:, e : e + 1], ALU.subtract, ALU.mult
+                        )
+                    else:
+                        nc.scalar.activation(
+                            z_rows[u][:, t, :], src, ACT.Identity, bias=shift[:, e : e + 1], scale=factor[:, e : e + 1]
+                        )
+
+        for u in range(2):
+            z_bf = sbuf("z_bf%d" % u, [P, HALF, PACK], BF16)
+            weave(nc.vector.tensor_copy, z_bf[:], z_rows[u][:])
+            z_codes = sbuf("z_codes%d" % u, [P, HALF], U32)
+            z_scales = sbuf("z_scales%d" % u, [P, HALF], U8)
+            quantize(z_codes[:], z_scales[:], z_bf[:].rearrange("p n j -> p (n j)"))
+            for b in range(2):
+                cols = slice(b * P, (b + 1) * P)
+                acc = ps.tile([P, HALF], F32, name="acc%d%d" % (u, b))
+                nc.tensor.matmul_mx(
+                    out=acc[:],
+                    lhsT=w2_codes[:, cols].bitcast(FP8X4),
+                    lhsT_scale=w2_scales[:, cols],
+                    rhs=z_codes[:].bitcast(FP8X4),
+                    rhs_scale=z_scales[:],
+                    start=True,
+                    stop=True,
+                )
+                res = sbuf("res%d%d" % (u, b), [P, HALF], F32)
+                dst = out[cols, u * HALF : (u + 1) * HALF]
+                if u == 1 and b == 1:
+                    nc.vector.tensor_copy(res[:], acc[:])
+                    nc.sync.dma_start(dst, res[:])
+                else:
+                    nc.scalar.copy(res[:], acc[:])
+                    nc.sync.dma_start(dst, res[:])

@@ -28,8 +28,8 @@ def tile_picked_inorm_none_e_kernel(tc, xT, w1, w2, gamma, offs, out):
         sb = ctx.enter_context(tc.tile_pool(name="sb", bufs=1))
         ps = ctx.enter_context(tc.psum_pool(name="ps", bufs=1))
 
-        def sbuf(name, shape, dtype):
-            return sb.tile(shape, dtype, name=name, align_bytes=64)
+        def sbuf(name, shape, dtype, tag=None):
+            return sb.tile(shape, dtype, name=name, tag=tag or name, align_bytes=64)
 
         def quantize(codes, scales, values):
             nc.vector.quantize_mx(out=codes.bitcast(FP8X4), scales=scales, in_=values)
@@ -53,18 +53,19 @@ def tile_picked_inorm_none_e_kernel(tc, xT, w1, w2, gamma, offs, out):
         nc.sync.dma_start(gain[:], gamma.rearrange("(p t) o -> p (t o)", t=PACK))
         for j in range(1, PACK):
             nc.sync.dma_start(x_raw[0][j][:], x_rows[0, j])
-        nc.sync.dma_start(w1_raw[0][:], w1_rows[0])
         for j in range(PACK):
             nc.sync.dma_start(x_raw[1][j][:], x_rows[1, j])
+        nc.sync.dma_start(w1_raw[0][:], w1_rows[0])
         nc.sync.dma_start(w1_raw[1][:], w1_rows[1])
         nc.sync.dma_start(w2_raw[:], w2.rearrange("(p j) n -> p j n", j=PACK))
 
         one = sbuf("one", [P, 1], F32)
         eps = sbuf("eps", [P, 1], F32)
         nc.vector.memset(one[:], 1.0)
-        nc.scalar.activation(eps[:], one[:], ACT.Sqrt, scale=EPS * EPS)
+        nc.scalar.activation(eps[:], one[:], ACT.Abs_reciprocal_sqrt, scale=1.0 / (EPS * EPS))
 
-        h_banks = [ps.tile([P, S], F32, name="h%d" % t) for t in range(PACK)]
+        h_banks = [ps.tile([P, S], F32, name="h%d" % t, tag="bank%d" % t) for t in range(PACK)]
+        xq = []
         for g in range(2):
             x_bf = sbuf("x_bf%d" % g, [P, S, PACK], BF16)
             x_pair = sbuf("x_pair%d" % g, [P, 2, S], BF16)
@@ -77,10 +78,14 @@ def tile_picked_inorm_none_e_kernel(tc, xT, w1, w2, gamma, offs, out):
             x_scales = sbuf("x_scales%d" % g, [P, S], U8)
             quantize(x_codes[:], x_scales[:], x_bf[:].rearrange("p n j -> p (n j)"))
 
+            xq.append((x_codes, x_scales))
+
+        for g in range(2):
+            x_codes, x_scales = xq[g]
             w1_bf = sbuf("w1_bf%d" % g, [P, PACK, P, PACK], BF16)
             dst = w1_bf[:].rearrange("p t m j -> p m j t")
             src = w1_raw[g][:].rearrange("p j (m t) -> p m j t", t=PACK)
-            split = W1_VECTOR_M if g == 1 else 0
+            split = W1_VECTOR_M if g == 1 else 72
             if split:
                 nc.vector.tensor_copy(dst[:, :split], src[:, :split])
             nc.scalar.copy(dst[:, split:], src[:, split:])
@@ -98,51 +103,69 @@ def tile_picked_inorm_none_e_kernel(tc, xT, w1, w2, gamma, offs, out):
                     stop=(g == 1),
                 )
 
-        w2_bf = sbuf("w2_bf", [P, N, PACK], BF16)
-        weave(nc.scalar.copy, w2_bf[:], w2_raw[:])
+        w2_bf = sbuf("w2_bf", [P, N, PACK], BF16, tag="w1_bf1")
+        nc.gpsimd.tensor_scalar(w2_bf[:], w2_raw[:].rearrange("p j n -> p n j"), 1.0, 0.0, ALU.mult, ALU.add)
+
+        h_rows = [sbuf("h_row%d" % t, [P, S], F32) for t in range(2)]
+        total = sbuf("total", [P, 1], F32)
+        squares = sbuf("squares", [P, S], BF16)
+        square_sum = sbuf("square_sum", [P, 1], F32)
+        moments = sbuf("moments", [P, PACK, 2], F32)
+        rstd = sbuf("rstd", [P, PACK], F32)
+        stats = sbuf("stats", [P, PACK - 1, 8], F32)
+        nc.scalar.activation(h_rows[0][:], h_banks[0][:], ACT.Identity, accum_out=total[:])
+        nc.scalar.activation(
+            squares[:], h_rows[0][:], ACT.Square, scale=-float(S), bias=total[:], accum_out=square_sum[:]
+        )
+        nc.scalar.activation(
+            rstd[:, 0:1], square_sum[:], ACT.Abs_reciprocal_sqrt, scale=1.0 / float(S) ** 3, bias=eps[:]
+        )
+        nc.scalar.activation(moments[:, 0, 0:1], total[:], ACT.Identity, scale=1.0 / S)
+        for t in range(1, PACK):
+            nc.vector.bn_stats(stats[:, t - 1, 0:6], h_banks[t][:])
+        nc.scalar.copy(h_rows[1][:], h_banks[1][:])
+        for t in range(1, PACK):
+            nc.vector.bn_aggr(moments[:, t, :], stats[:, t - 1, 0:6])
+        nc.scalar.activation(rstd[:, 1:], moments[:, 1:, 1], ACT.Abs_reciprocal_sqrt, bias=eps[:])
+
         w2_codes = sbuf("w2_codes", [P, N], U32)
         w2_scales = sbuf("w2_scales", [P, N], U8)
         quantize(w2_codes[:], w2_scales[:], w2_bf[:].rearrange("p n j -> p (n j)"))
 
-        z_rows = [sbuf("z_rows%d" % u, [P, PACK, HALF], BF16) for u in range(2)]
-        for pair in range(2):
-            ts = slice(2 * pair, 2 * pair + 2)
-            stats = sbuf("stats%d" % pair, [P, 2, 8], F32)
-            moments = sbuf("moments%d" % pair, [P, 2, 2], F32)
-            for e in range(2):
-                nc.vector.bn_stats(stats[:, e, 0:6], h_banks[2 * pair + e][:])
-            for e in range(2):
-                nc.vector.bn_aggr(moments[:, e, :], stats[:, e, 0:6])
-            std = sbuf("std%d" % pair, [P, 2], F32)
-            nc.scalar.activation(std[:], moments[:, :, 1], ACT.Sqrt, bias=eps[:])
-            rstd = sbuf("rstd%d" % pair, [P, 2], F32)
-            nc.vector.reciprocal(rstd[:], std[:])
-            factor = sbuf("factor%d" % pair, [P, 2], F32)
-            nc.vector.tensor_tensor(factor[:], rstd[:], gain[:, ts], ALU.mult)
-            shift = sbuf("shift%d" % pair, [P, 2], F32)
-            nc.vector.scalar_tensor_tensor(shift[:], moments[:, :, 0], -1.0, factor[:], ALU.mult, ALU.mult)
-            for u in range(2):
-                for e in range(2):
-                    t = 2 * pair + e
-                    src = h_banks[t][:, u * HALF : (u + 1) * HALF]
-                    if t == 2 and u == 0:
-                        nc.vector.tensor_scalar(
-                            z_rows[u][:, t, :], src, moments[:, e, 0:1], factor[:, e : e + 1], ALU.subtract, ALU.mult
-                        )
-                    else:
-                        nc.scalar.activation(
-                            z_rows[u][:, t, :], src, ACT.Identity, bias=shift[:, e : e + 1], scale=factor[:, e : e + 1]
-                        )
+        factor = sbuf("factor", [P, PACK], F32)
+        nc.vector.tensor_tensor(factor[:], rstd[:], gain[:], ALU.mult)
+        shift = sbuf("shift", [P, 2], F32)
+        nc.vector.scalar_tensor_tensor(shift[:], moments[:, 2:, 0], -1.0, factor[:, 2:], ALU.mult, ALU.mult)
 
-        for u in range(2):
-            z_bf = sbuf("z_bf%d" % u, [P, HALF, PACK], BF16)
-            weave(nc.vector.tensor_copy, z_bf[:], z_rows[u][:])
-            z_codes = sbuf("z_codes%d" % u, [P, HALF], U32)
-            z_scales = sbuf("z_scales%d" % u, [P, HALF], U8)
+        z_rows = [sbuf("z_rows%d" % u, [P, PACK, HALF], BF16) for u in range(2)]
+
+        def normalise_vector(u, t):
+            src = (h_rows[t] if t < 2 else h_banks[t])[:, u * HALF : (u + 1) * HALF]
+            nc.vector.tensor_scalar(
+                z_rows[u][:, t, :], src, moments[:, t, 0:1], factor[:, t : t + 1], ALU.subtract, ALU.mult
+            )
+
+        def normalise_scalar(u, t):
+            nc.scalar.activation(
+                z_rows[u][:, t, :],
+                h_banks[t][:, u * HALF : (u + 1) * HALF],
+                ACT.Identity,
+                bias=shift[:, t - 2 : t - 1],
+                scale=factor[:, t : t + 1],
+            )
+
+        def quantize_z(name, z_bf, width):
+            z_codes = sbuf("z_codes" + name, [P, width], U32)
+            z_scales = sbuf("z_scales" + name, [P, width], U8)
             quantize(z_codes[:], z_scales[:], z_bf[:].rearrange("p n j -> p (n j)"))
+            return z_codes, z_scales
+
+        def second_layer(name, z_quantized, first, width, banks):
+            z_codes, z_scales = z_quantized
+            res = sbuf("res" + name, [P, 2, width], F32)
             for b in range(2):
                 cols = slice(b * P, (b + 1) * P)
-                acc = ps.tile([P, HALF], F32, name="acc%d%d" % (u, b))
+                acc = ps.tile([P, width], F32, name="acc%s%d" % (name, b), tag="bank%d" % banks[b])
                 nc.tensor.matmul_mx(
                     out=acc[:],
                     lhsT=w2_codes[:, cols].bitcast(FP8X4),
@@ -152,11 +175,26 @@ def tile_picked_inorm_none_e_kernel(tc, xT, w1, w2, gamma, offs, out):
                     start=True,
                     stop=True,
                 )
-                res = sbuf("res%d%d" % (u, b), [P, HALF], F32)
-                dst = out[cols, u * HALF : (u + 1) * HALF]
-                if u == 1 and b == 1:
-                    nc.vector.tensor_copy(res[:], acc[:])
-                    nc.sync.dma_start(dst, res[:])
-                else:
-                    nc.scalar.copy(res[:], acc[:])
-                    nc.sync.dma_start(dst, res[:])
+                (nc.vector.tensor_copy if b == 0 else nc.scalar.copy)(res[:, b, :], acc[:])
+            nc.sync.dma_start(out[:, first : first + width].rearrange("(b p) n -> p b n", p=P), res[:])
+
+        quarter = HALF // 2
+        for t in range(3):
+            normalise_vector(0, t)
+        normalise_scalar(0, 3)
+        normalise_scalar(1, 3)
+        normalise_scalar(1, 2)
+        z_a = sbuf("z_a", [P, HALF, PACK], BF16)
+        z_b = sbuf("z_b", [P, quarter, PACK], BF16)
+        z_c = sbuf("z_c", [P, quarter, PACK], BF16)
+        weave(nc.vector.tensor_copy, z_a[:], z_rows[0][:])
+        for t in range(2):
+            normalise_vector(1, t)
+        q_a = quantize_z("a", z_a, HALF)
+        weave(nc.scalar.copy, z_c[:], z_rows[1][:, :, quarter:])
+        weave(nc.vector.tensor_copy, z_b[:], z_rows[1][:, :, :quarter])
+        q_c = quantize_z("c", z_c, quarter)
+        q_b = quantize_z("b", z_b, quarter)
+        second_layer("a", q_a, 0, HALF, (4, 5))
+        second_layer("c", q_c, HALF + quarter, quarter, (6, 7))
+        second_layer("b", q_b, HALF, quarter, (0, 1))

@@ -19,6 +19,8 @@ P = 128
 PACK = 4
 K_PASS = P * PACK
 HALF = S // 2
+CHUNK = 128
+CHUNKS = S // CHUNK
 W1_VECTOR_M = 88
 
 
@@ -40,7 +42,7 @@ def tile_picked_inorm_none_e_kernel(tc, xT, w1, w2, gamma, offs, out):
                 src.rearrange("p j (c i) -> p c j i", i=4),
             )
 
-        x_rows = xT.rearrange("(g p j) t -> g j p t", p=P, j=PACK)
+        x_rows = xT.rearrange("(g p j) t -> g p j t", p=P, j=PACK)
         w1_rows = w1.rearrange("(g p j) c -> g p j c", p=P, j=PACK)
         x_raw = [[sbuf("x_raw%d%d" % (g, j), [P, T], F32) for j in range(PACK)] for g in range(2)]
         w1_raw = [sbuf("w1_raw%d" % g, [P, PACK, H], F32) for g in range(2)]
@@ -48,15 +50,15 @@ def tile_picked_inorm_none_e_kernel(tc, xT, w1, w2, gamma, offs, out):
         offsets = sb.tile([P, S // 16], U16, name="offsets")
         gain = sbuf("gain", [P, PACK], F32)
 
-        nc.sync.dma_start(x_raw[0][0][:], x_rows[0, 0])
+        nc.sync.dma_start(x_raw[0][0][:], x_rows[0, :, 0])
         nc.sync.dma_start(offsets[:], offs)
         nc.sync.dma_start(gain[:], gamma.rearrange("(p t) o -> p (t o)", t=PACK))
         for j in range(1, PACK):
-            nc.sync.dma_start(x_raw[0][j][:], x_rows[0, j])
+            nc.sync.dma_start(x_raw[0][j][:], x_rows[0, :, j])
         for j in range(PACK):
-            nc.sync.dma_start(x_raw[1][j][:], x_rows[1, j])
-        nc.sync.dma_start(w1_raw[0][:], w1_rows[0])
-        nc.sync.dma_start(w1_raw[1][:], w1_rows[1])
+            nc.sync.dma_start(x_raw[1][j][:], x_rows[1, :, j])
+        for g in range(2):
+            nc.sync.dma_start(w1_raw[g][:], w1_rows[g])
         nc.sync.dma_start(w2_raw[:], w2.rearrange("(p j) n -> p j n", j=PACK))
 
         one = sbuf("one", [P, 1], F32)
@@ -65,29 +67,19 @@ def tile_picked_inorm_none_e_kernel(tc, xT, w1, w2, gamma, offs, out):
         nc.scalar.activation(eps[:], one[:], ACT.Abs_reciprocal_sqrt, scale=1.0 / (EPS * EPS))
 
         h_banks = [ps.tile([P, S], F32, name="h%d" % t, tag="bank%d" % t) for t in range(PACK)]
-        xq = []
-        for g in range(2):
-            x_bf = sbuf("x_bf%d" % g, [P, S, PACK], BF16)
-            x_pair = sbuf("x_pair%d" % g, [P, 2, S], BF16)
-            for j in range(2):
-                nc.vector.tensor_copy(x_pair[:, j, :], x_raw[g][j][:].indirect(offsets[:]))
-            weave(nc.scalar.copy, x_bf[:, :, 0:2], x_pair[:])
-            for j in range(2, PACK):
-                nc.vector.tensor_copy(x_bf[:, :, j], x_raw[g][j][:].indirect(offsets[:]))
-            x_codes = sbuf("x_codes%d" % g, [P, S], U32)
+        def quantize_x(g, x_bf, tag=None):
+            x_codes = sbuf("x_codes%d" % g, [P, S], U32, tag=tag)
             x_scales = sbuf("x_scales%d" % g, [P, S], U8)
             quantize(x_codes[:], x_scales[:], x_bf[:].rearrange("p n j -> p (n j)"))
+            return x_codes, x_scales
 
-            xq.append((x_codes, x_scales))
-
-        for g in range(2):
-            x_codes, x_scales = xq[g]
+        def first_layer_pass(g, x_quantized):
+            x_codes, x_scales = x_quantized
             w1_bf = sbuf("w1_bf%d" % g, [P, PACK, P, PACK], BF16)
             dst = w1_bf[:].rearrange("p t m j -> p m j t")
             src = w1_raw[g][:].rearrange("p j (m t) -> p m j t", t=PACK)
-            split = W1_VECTOR_M if g == 1 else 72
-            if split:
-                nc.vector.tensor_copy(dst[:, :split], src[:, :split])
+            split = W1_VECTOR_M
+            nc.vector.tensor_copy(dst[:, :split], src[:, :split])
             nc.scalar.copy(dst[:, split:], src[:, split:])
             for t in range(PACK):
                 w1_codes = sbuf("w1_codes%d%d" % (g, t), [P, P], U32)
@@ -103,10 +95,31 @@ def tile_picked_inorm_none_e_kernel(tc, xT, w1, w2, gamma, offs, out):
                     stop=(g == 1),
                 )
 
+        x_bf = [sbuf("x_bf%d" % g, [P, S, PACK], BF16) for g in range(2)]
+
+        def gather_rows01(g):
+            picked = sbuf("picked%d" % g, [P, 2, S], BF16)
+            for j in range(2):
+                nc.vector.tensor_copy(picked[:, j, :], x_raw[g][j][:].indirect(offsets[:]))
+            weave(nc.scalar.copy, x_bf[g][:, :, 0:2], picked[:])
+
+        def gather_row(g, j):
+            nc.vector.tensor_copy(x_bf[g][:, :, j], x_raw[g][j][:].indirect(offsets[:]))
+
+        gather_rows01(0)
+        gather_row(0, 2)
+        gather_row(0, 3)
+        x_q0 = quantize_x(0, x_bf[0])
+        gather_rows01(1)
+        gather_row(1, 2)
+        gather_row(1, 3)
+        first_layer_pass(0, x_q0)
+        first_layer_pass(1, quantize_x(1, x_bf[1], tag="w1_raw0"))
+
         w2_bf = sbuf("w2_bf", [P, N, PACK], BF16, tag="w1_bf1")
         nc.gpsimd.tensor_scalar(w2_bf[:], w2_raw[:].rearrange("p j n -> p n j"), 1.0, 0.0, ALU.mult, ALU.add)
 
-        h_rows = [sbuf("h_row%d" % t, [P, S], F32) for t in range(2)]
+        h_rows = [sbuf("h_row%d" % t, [P, width], F32) for t, width in enumerate((S, S, HALF))]
         total = sbuf("total", [P, 1], F32)
         squares = sbuf("squares", [P, S], BF16)
         square_sum = sbuf("square_sum", [P, 1], F32)
@@ -121,53 +134,70 @@ def tile_picked_inorm_none_e_kernel(tc, xT, w1, w2, gamma, offs, out):
             rstd[:, 0:1], square_sum[:], ACT.Abs_reciprocal_sqrt, scale=1.0 / float(S) ** 3, bias=eps[:]
         )
         nc.scalar.activation(moments[:, 0, 0:1], total[:], ACT.Identity, scale=1.0 / S)
-        for t in range(1, PACK):
-            nc.vector.bn_stats(stats[:, t - 1, 0:6], h_banks[t][:])
+        for t in range(1, PACK + 1):
+            if t < PACK:
+                nc.vector.bn_stats(stats[:, t - 1, 0:6], h_banks[t][:])
+            if t > 1:
+                nc.vector.bn_aggr(moments[:, t - 1, :], stats[:, t - 2, 0:6])
         nc.scalar.copy(h_rows[1][:], h_banks[1][:])
-        for t in range(1, PACK):
-            nc.vector.bn_aggr(moments[:, t, :], stats[:, t - 1, 0:6])
+        nc.scalar.copy(h_rows[2][:], h_banks[2][:, :HALF])
         nc.scalar.activation(rstd[:, 1:], moments[:, 1:, 1], ACT.Abs_reciprocal_sqrt, bias=eps[:])
 
         w2_codes = sbuf("w2_codes", [P, N], U32)
         w2_scales = sbuf("w2_scales", [P, N], U8)
         quantize(w2_codes[:], w2_scales[:], w2_bf[:].rearrange("p n j -> p (n j)"))
 
+        warm = ps.tile([P, S], F32, name="warm", tag="bank6")
+        for b in range(2):
+            cols = slice(b * P, (b + 1) * P)
+            nc.tensor.matmul_mx(
+                out=warm[:],
+                lhsT=w2_codes[:, cols].bitcast(FP8X4),
+                lhsT_scale=w2_scales[:, cols],
+                rhs=x_q0[0][:].bitcast(FP8X4),
+                rhs_scale=x_q0[1][:],
+                start=True,
+                stop=True,
+            )
+
         factor = sbuf("factor", [P, PACK], F32)
         nc.vector.tensor_tensor(factor[:], rstd[:], gain[:], ALU.mult)
         shift = sbuf("shift", [P, 2], F32)
         nc.vector.scalar_tensor_tensor(shift[:], moments[:, 2:, 0], -1.0, factor[:, 2:], ALU.mult, ALU.mult)
 
-        z_rows = [sbuf("z_rows%d" % u, [P, PACK, HALF], BF16) for u in range(2)]
-
-        def normalise_vector(u, t):
-            src = (h_rows[t] if t < 2 else h_banks[t])[:, u * HALF : (u + 1) * HALF]
+        z_rows = sbuf("z_rows", [P, PACK, S], BF16)
+        first_half, second_half = slice(0, HALF), slice(HALF, S)
+        for t, cols in ((0, slice(0, S)), (1, slice(0, S)), (2, first_half)):
             nc.vector.tensor_scalar(
-                z_rows[u][:, t, :], src, moments[:, t, 0:1], factor[:, t : t + 1], ALU.subtract, ALU.mult
+                z_rows[:, t, cols], h_rows[t][:], moments[:, t, 0:1], factor[:, t : t + 1], ALU.subtract, ALU.mult
             )
-
-        def normalise_scalar(u, t):
+        for t, cols in ((3, first_half), (2, second_half), (3, second_half)):
             nc.scalar.activation(
-                z_rows[u][:, t, :],
-                h_banks[t][:, u * HALF : (u + 1) * HALF],
+                z_rows[:, t, cols],
+                h_banks[t][:, cols],
                 ACT.Identity,
                 bias=shift[:, t - 2 : t - 1],
                 scale=factor[:, t : t + 1],
             )
 
-        def quantize_z(name, z_bf, width):
-            z_codes = sbuf("z_codes" + name, [P, width], U32)
-            z_scales = sbuf("z_scales" + name, [P, width], U8)
-            quantize(z_codes[:], z_scales[:], z_bf[:].rearrange("p n j -> p (n j)"))
-            return z_codes, z_scales
+        z_bf = [sbuf("z_bf%d" % c, [P, CHUNK, PACK], BF16) for c in range(CHUNKS)]
 
-        def second_layer(name, z_quantized, first, width, banks):
-            z_codes, z_scales = z_quantized
-            res = sbuf("res" + name, [P, 2, width], F32)
+        def weave_z(c, engine_copy):
+            weave(engine_copy, z_bf[c][:], z_rows[:, :, c * CHUNK : (c + 1) * CHUNK])
+
+        def second_layer(c, last):
+            z_codes = sbuf("z_codes%d" % c, [P, CHUNK], U32)
+            z_scales = sbuf("z_scales%d" % c, [P, CHUNK], U8)
+            quantize(z_codes[:], z_scales[:], z_bf[c][:].rearrange("p n j -> p (n j)"))
+            if last:
+                accs = [ps.tile([P, CHUNK], F32, name="acc_last%d" % b, tag="bank%d" % b)[:] for b in range(2)]
+            else:
+                acc = ps.tile([P, 2, CHUNK], F32, name="acc%d" % c, tag="bank%d" % (PACK + c))
+                accs = [acc[:, b, :] for b in range(2)] + [acc[:]]
             for b in range(2):
                 cols = slice(b * P, (b + 1) * P)
-                acc = ps.tile([P, width], F32, name="acc%s%d" % (name, b), tag="bank%d" % banks[b])
                 nc.tensor.matmul_mx(
-                    out=acc[:],
+                    out=accs[b],
                     lhsT=w2_codes[:, cols].bitcast(FP8X4),
                     lhsT_scale=w2_scales[:, cols],
                     rhs=z_codes[:].bitcast(FP8X4),
@@ -175,26 +205,24 @@ def tile_picked_inorm_none_e_kernel(tc, xT, w1, w2, gamma, offs, out):
                     start=True,
                     stop=True,
                 )
-                (nc.vector.tensor_copy if b == 0 else nc.scalar.copy)(res[:, b, :], acc[:])
-            nc.sync.dma_start(out[:, first : first + width].rearrange("(b p) n -> p b n", p=P), res[:])
+            return accs
 
-        quarter = HALF // 2
-        for t in range(3):
-            normalise_vector(0, t)
-        normalise_scalar(0, 3)
-        normalise_scalar(1, 3)
-        normalise_scalar(1, 2)
-        z_a = sbuf("z_a", [P, HALF, PACK], BF16)
-        z_b = sbuf("z_b", [P, quarter, PACK], BF16)
-        z_c = sbuf("z_c", [P, quarter, PACK], BF16)
-        weave(nc.vector.tensor_copy, z_a[:], z_rows[0][:])
-        for t in range(2):
-            normalise_vector(1, t)
-        q_a = quantize_z("a", z_a, HALF)
-        weave(nc.scalar.copy, z_c[:], z_rows[1][:, :, quarter:])
-        weave(nc.vector.tensor_copy, z_b[:], z_rows[1][:, :, :quarter])
-        q_c = quantize_z("c", z_c, quarter)
-        q_b = quantize_z("b", z_b, quarter)
-        second_layer("a", q_a, 0, HALF, (4, 5))
-        second_layer("c", q_c, HALF + quarter, quarter, (6, 7))
-        second_layer("b", q_b, HALF, quarter, (0, 1))
+        def store(c, copies):
+            res = sbuf("res%d" % c, [P, 2, CHUNK], F32)
+            for engine_copy, rows, acc in copies:
+                engine_copy(res[:, rows], acc)
+            nc.sync.dma_start(out[:, c * CHUNK : (c + 1) * CHUNK].rearrange("(b p) n -> p b n", p=P), res[:])
+
+        weave_z(3, nc.scalar.copy)
+        weave_z(0, nc.vector.tensor_copy)
+        weave_z(1, nc.vector.tensor_copy)
+        acc0 = second_layer(0, False)
+        weave_z(2, nc.vector.tensor_copy)
+        acc1 = second_layer(1, False)
+        acc3 = second_layer(3, False)
+        acc2 = second_layer(2, True)
+        both = slice(0, 2)
+        store(0, [(nc.scalar.copy, both, acc0[2])])
+        store(1, [(nc.scalar.copy, both, acc1[2])])
+        store(3, [(nc.vector.tensor_copy, both, acc3[2])])
+        store(2, [(nc.scalar.copy, 0, acc2[0]), (nc.vector.tensor_copy, 1, acc2[1])])

@@ -21,7 +21,7 @@ K_PASS = P * PACK
 HALF = S // 2
 CHUNK = 128
 CHUNKS = S // CHUNK
-W1_VECTOR_M = 88
+W1_VECTOR_M = (88, 80)
 
 
 def tile_picked_inorm_none_e_kernel(tc, xT, w1, w2, gamma, offs, out):
@@ -52,7 +52,6 @@ def tile_picked_inorm_none_e_kernel(tc, xT, w1, w2, gamma, offs, out):
 
         nc.sync.dma_start(x_raw[0][0][:], x_rows[0, :, 0])
         nc.sync.dma_start(offsets[:], offs)
-        nc.sync.dma_start(gain[:], gamma.rearrange("(p t) o -> p (t o)", t=PACK))
         for j in range(1, PACK):
             nc.sync.dma_start(x_raw[0][j][:], x_rows[0, :, j])
         for j in range(PACK):
@@ -60,6 +59,7 @@ def tile_picked_inorm_none_e_kernel(tc, xT, w1, w2, gamma, offs, out):
         for g in range(2):
             nc.sync.dma_start(w1_raw[g][:], w1_rows[g])
         nc.sync.dma_start(w2_raw[:], w2.rearrange("(p j) n -> p j n", j=PACK))
+        nc.sync.dma_start(gain[:], gamma.rearrange("(p t) o -> p (t o)", t=PACK))
 
         one = sbuf("one", [P, 1], F32)
         eps = sbuf("eps", [P, 1], F32)
@@ -78,7 +78,7 @@ def tile_picked_inorm_none_e_kernel(tc, xT, w1, w2, gamma, offs, out):
             w1_bf = sbuf("w1_bf%d" % g, [P, PACK, P, PACK], BF16)
             dst = w1_bf[:].rearrange("p t m j -> p m j t")
             src = w1_raw[g][:].rearrange("p j (m t) -> p m j t", t=PACK)
-            split = W1_VECTOR_M
+            split = W1_VECTOR_M[g]
             nc.vector.tensor_copy(dst[:, :split], src[:, :split])
             nc.scalar.copy(dst[:, split:], src[:, split:])
             for t in range(PACK):
@@ -97,22 +97,16 @@ def tile_picked_inorm_none_e_kernel(tc, xT, w1, w2, gamma, offs, out):
 
         x_bf = [sbuf("x_bf%d" % g, [P, S, PACK], BF16) for g in range(2)]
 
-        def gather_rows01(g):
-            picked = sbuf("picked%d" % g, [P, 2, S], BF16)
-            for j in range(2):
-                nc.vector.tensor_copy(picked[:, j, :], x_raw[g][j][:].indirect(offsets[:]))
-            weave(nc.scalar.copy, x_bf[g][:, :, 0:2], picked[:])
+        def gather(name, g, rows):
+            picked = sbuf(name, [P, len(rows), S], BF16)
+            for i, j in enumerate(rows):
+                nc.vector.tensor_copy(picked[:, i, :], x_raw[g][j][:].indirect(offsets[:]))
+            return picked
 
-        def gather_row(g, j):
-            nc.vector.tensor_copy(x_bf[g][:, :, j], x_raw[g][j][:].indirect(offsets[:]))
-
-        gather_rows01(0)
-        gather_row(0, 2)
-        gather_row(0, 3)
+        weave(nc.scalar.copy, x_bf[0][:], gather("picked0", 0, range(PACK))[:])
+        weave(nc.scalar.copy, x_bf[1][:, :, 0:2], gather("picked1a", 1, (0, 1))[:])
         x_q0 = quantize_x(0, x_bf[0])
-        gather_rows01(1)
-        gather_row(1, 2)
-        gather_row(1, 3)
+        weave(nc.vector.tensor_copy, x_bf[1][:, :, 2:4], gather("picked1b", 1, (2, 3))[:])
         first_layer_pass(0, x_q0)
         first_layer_pass(1, quantize_x(1, x_bf[1], tag="w1_raw0"))
 
@@ -146,19 +140,6 @@ def tile_picked_inorm_none_e_kernel(tc, xT, w1, w2, gamma, offs, out):
         w2_codes = sbuf("w2_codes", [P, N], U32)
         w2_scales = sbuf("w2_scales", [P, N], U8)
         quantize(w2_codes[:], w2_scales[:], w2_bf[:].rearrange("p n j -> p (n j)"))
-
-        warm = ps.tile([P, S], F32, name="warm", tag="bank6")
-        for b in range(2):
-            cols = slice(b * P, (b + 1) * P)
-            nc.tensor.matmul_mx(
-                out=warm[:],
-                lhsT=w2_codes[:, cols].bitcast(FP8X4),
-                lhsT_scale=w2_scales[:, cols],
-                rhs=x_q0[0][:].bitcast(FP8X4),
-                rhs_scale=x_q0[1][:],
-                start=True,
-                stop=True,
-            )
 
         factor = sbuf("factor", [P, PACK], F32)
         nc.vector.tensor_tensor(factor[:], rstd[:], gain[:], ALU.mult)
@@ -223,6 +204,6 @@ def tile_picked_inorm_none_e_kernel(tc, xT, w1, w2, gamma, offs, out):
         acc2 = second_layer(2, True)
         both = slice(0, 2)
         store(0, [(nc.scalar.copy, both, acc0[2])])
-        store(1, [(nc.scalar.copy, both, acc1[2])])
-        store(3, [(nc.vector.tensor_copy, both, acc3[2])])
-        store(2, [(nc.scalar.copy, 0, acc2[0]), (nc.vector.tensor_copy, 1, acc2[1])])
+        store(1, [(nc.vector.tensor_copy, both, acc1[2])])
+        store(3, [(nc.scalar.copy, both, acc3[2])])
+        store(2, [(nc.vector.tensor_copy, 0, acc2[0]), (nc.vector.tensor_copy, 1, acc2[1])])

@@ -53,13 +53,13 @@ def tile_picked_inorm_none_e_kernel(tc, xT, w1, w2, gamma, offs, out):
         nc.sync.dma_start(x_raw[0][0][:], x_rows[0, :, 0])
         nc.sync.dma_start(offsets[:], offs)
         for j in range(1, PACK):
-            nc.sync.dma_start(x_raw[0][j][:], x_rows[0, :, j])
+            (nc.scalar if j % 2 else nc.sync).dma_start(x_raw[0][j][:], x_rows[0, :, j])
+        nc.scalar.dma_start(gain[:], gamma.rearrange("(p t) o -> p (t o)", t=PACK))
         for j in range(PACK):
             nc.sync.dma_start(x_raw[1][j][:], x_rows[1, :, j])
         for g in range(2):
             nc.sync.dma_start(w1_raw[g][:], w1_rows[g])
         nc.sync.dma_start(w2_raw[:], w2.rearrange("(p j) n -> p j n", j=PACK))
-        nc.sync.dma_start(gain[:], gamma.rearrange("(p t) o -> p (t o)", t=PACK))
 
         one = sbuf("one", [P, 1], F32)
         eps = sbuf("eps", [P, 1], F32)
@@ -106,7 +106,8 @@ def tile_picked_inorm_none_e_kernel(tc, xT, w1, w2, gamma, offs, out):
         weave(nc.scalar.copy, x_bf[0][:], gather("picked0", 0, range(PACK))[:])
         weave(nc.scalar.copy, x_bf[1][:, :, 0:2], gather("picked1a", 1, (0, 1))[:])
         x_q0 = quantize_x(0, x_bf[0])
-        weave(nc.vector.tensor_copy, x_bf[1][:, :, 2:4], gather("picked1b", 1, (2, 3))[:])
+        for j in (2, 3):
+            nc.vector.tensor_copy(x_bf[1][:, :, j], x_raw[1][j][:].indirect(offsets[:]))
         first_layer_pass(0, x_q0)
         first_layer_pass(1, quantize_x(1, x_bf[1], tag="w1_raw0"))
 

from contextlib import ExitStack

import concourse.mybir as mybir

K, T, S, H, N = 1024, 2048, 512, 512, 256
FLOPS = 2 * K * H * S + 2 * H * N * S
EPS = 1e-5

F32 = mybir.dt.float32
BF16 = mybir.dt.bfloat16
U32 = mybir.dt.uint32
U16 = mybir.dt.uint16
U8 = mybir.dt.uint8
FP8X4 = mybir.dt.float8_e4m3fn_x4
ALU = mybir.AluOpType
ACT = mybir.ActivationFunctionType

P = 128
PACK = 4
K_PASS = P * PACK
HALF = S // 2
CHUNK = 128
CHUNKS = S // CHUNK
W1_VECTOR_M = (88, 80)


def tile_picked_inorm_none_e_kernel(tc, xT, w1, w2, gamma, offs, out):
    nc = tc.nc
    with ExitStack() as ctx:
        sb = ctx.enter_context(tc.tile_pool(name="sb", bufs=1))
        ps = ctx.enter_context(tc.psum_pool(name="ps", bufs=1))

        def sbuf(name, shape, dtype, tag=None):
            return sb.tile(shape, dtype, name=name, tag=tag or name, align_bytes=64)

        def quantize(codes, scales, values):
            nc.vector.quantize_mx(out=codes.bitcast(FP8X4), scales=scales, in_=values)

        def weave(engine_copy, dst, src):
            engine_copy(
                dst.rearrange("p (c i) j -> p c j i", i=4),
                src.rearrange("p j (c i) -> p c j i", i=4),
            )

        x_rows = xT.rearrange("(g p j) t -> g p j t", p=P, j=PACK)
        w1_rows = w1.rearrange("(g p j) c -> g p j c", p=P, j=PACK)
        x_raw = [[sbuf("x_raw%d%d" % (g, j), [P, T], F32) for j in range(PACK)] for g in range(2)]
        w1_raw = [sbuf("w1_raw%d" % g, [P, PACK, H], F32) for g in range(2)]
        w2_raw = sbuf("w2_raw", [P, PACK, N], F32)
        offsets = sb.tile([P, S // 16], U16, name="offsets")
        gain = sbuf("gain", [P, PACK], F32)

        nc.sync.dma_start(x_raw[0][0][:], x_rows[0, :, 0])
        nc.sync.dma_start(offsets[:], offs)
        for j in range(1, PACK):
            (nc.scalar if j % 2 else nc.sync).dma_start(x_raw[0][j][:], x_rows[0, :, j])
        nc.scalar.dma_start(gain[:], gamma.rearrange("(p t) o -> p (t o)", t=PACK))
        for j in range(PACK):
            nc.sync.dma_start(x_raw[1][j][:], x_rows[1, :, j])
        for g in range(2):
            nc.sync.dma_start(w1_raw[g][:], w1_rows[g])
        nc.sync.dma_start(w2_raw[:], w2.rearrange("(p j) n -> p j n", j=PACK))

        one = sbuf("one", [P, 1], F32)
        eps = sbuf("eps", [P, 1], F32)
        nc.vector.memset(one[:], 1.0)
        nc.scalar.activation(eps[:], one[:], ACT.Abs_reciprocal_sqrt, scale=1.0 / (EPS * EPS))

        h_banks = [ps.tile([P, S], F32, name="h%d" % t, tag="bank%d" % t) for t in range(PACK)]
        def quantize_x(g, x_bf, tag=None):
            x_codes = sbuf("x_codes%d" % g, [P, S], U32, tag=tag)
            x_scales = sbuf("x_scales%d" % g, [P, S], U8)
            quantize(x_codes[:], x_scales[:], x_bf[:].rearrange("p n j -> p (n j)"))
            return x_codes, x_scales

        def first_layer_pass(g, x_quantized):
            x_codes, x_scales = x_quantized
            w1_bf = sbuf("w1_bf%d" % g, [P, PACK, P, PACK], BF16)
            dst = w1_bf[:].rearrange("p t m j -> p m j t")
            src = w1_raw[g][:].rearrange("p j (m t) -> p m j t", t=PACK)
            split = W1_VECTOR_M[g]
            nc.vector.tensor_copy(dst[:, :split], src[:, :split])
            nc.scalar.copy(dst[:, split:], src[:, split:])
            for t in range(PACK):
                w1_codes = sbuf("w1_codes%d%d" % (g, t), [P, P], U32)
                w1_scales = sbuf("w1_scales%d%d" % (g, t), [P, P], U8)
                quantize(w1_codes[:], w1_scales[:], w1_bf[:, t].rearrange("p m j -> p (m j)"))
                nc.tensor.matmul_mx(
                    out=h_banks[t][:],
                    lhsT=w1_codes[:].bitcast(FP8X4),
                    lhsT_scale=w1_scales[:],
                    rhs=x_codes[:].bitcast(FP8X4),
                    rhs_scale=x_scales[:],
                    start=(g == 0),
                    stop=(g == 1),
                )

        x_bf = [sbuf("x_bf%d" % g, [P, S, PACK], BF16) for g in range(2)]

        def gather(name, g, rows):
            picked = sbuf(name, [P, len(rows), S], BF16)
            for i, j in enumerate(rows):
                nc.vector.tensor_copy(picked[:, i, :], x_raw[g][j][:].indirect(offsets[:]))
            return picked

        weave(nc.scalar.copy, x_bf[0][:], gather("picked0", 0, range(PACK))[:])
        weave(nc.scalar.copy, x_bf[1][:, :, 0:2], gather("picked1a", 1, (0, 1))[:])
        x_q0 = quantize_x(0, x_bf[0])
        for j in (2, 3):
            nc.vector.tensor_copy(x_bf[1][:, :, j], x_raw[1][j][:].indirect(offsets[:]))
        first_layer_pass(0, x_q0)
        first_layer_pass(1, quantize_x(1, x_bf[1], tag="w1_raw0"))

        w2_bf = sbuf("w2_bf", [P, N, PACK], BF16, tag="w1_bf1")
        nc.gpsimd.tensor_scalar(w2_bf[:], w2_raw[:].rearrange("p j n -> p n j"), 1.0, 0.0, ALU.mult, ALU.add)

        h_rows = [sbuf("h_row%d" % t, [P, width], F32) for t, width in enumerate((S, S, HALF))]
        total = sbuf("total", [P, 1], F32)
        squares = sbuf("squares", [P, S], BF16)
        square_sum = sbuf("square_sum", [P, 1], F32)
        moments = sbuf("moments", [P, PACK, 2], F32)
        rstd = sbuf("rstd", [P, PACK], F32)
        stats = sbuf("stats", [P, PACK - 1, 8], F32)
        nc.scalar.activation(h_rows[0][:], h_banks[0][:], ACT.Identity, accum_out=total[:])
        nc.scalar.activation(
            squares[:], h_rows[0][:], ACT.Square, scale=-float(S), bias=total[:], accum_out=square_sum[:]
        )
        nc.scalar.activation(
            rstd[:, 0:1], square_sum[:], ACT.Abs_reciprocal_sqrt, scale=1.0 / float(S) ** 3, bias=eps[:]
        )
        nc.scalar.activation(moments[:, 0, 0:1], total[:], ACT.Identity, scale=1.0 / S)
        for t in range(1, PACK + 1):
            if t < PACK:
                nc.vector.bn_stats(stats[:, t - 1, 0:6], h_banks[t][:])
            if t > 1:
                nc.vector.bn_aggr(moments[:, t - 1, :], stats[:, t - 2, 0:6])
        nc.scalar.copy(h_rows[1][:], h_banks[1][:])
        nc.scalar.copy(h_rows[2][:], h_banks[2][:, :HALF])
        nc.scalar.activation(rstd[:, 1:], moments[:, 1:, 1], ACT.Abs_reciprocal_sqrt, bias=eps[:])

        w2_codes = sbuf("w2_codes", [P, N], U32)
        w2_scales = sbuf("w2_scales", [P, N], U8)
        quantize(w2_codes[:], w2_scales[:], w2_bf[:].rearrange("p n j -> p (n j)"))

        factor = sbuf("factor", [P, PACK], F32)
        nc.vector.tensor_tensor(factor[:], rstd[:], gain[:], ALU.mult)
        shift = sbuf("shift", [P, 2], F32)
        nc.vector.scalar_tensor_tensor(shift[:], moments[:, 2:, 0], -1.0, factor[:, 2:], ALU.mult, ALU.mult)

        z_rows = sbuf("z_rows", [P, PACK, S], BF16)
        first_half, second_half = slice(0, HALF), slice(HALF, S)
        for t, cols in ((0, slice(0, S)), (1, slice(0, S)), (2, first_half)):
            nc.vector.tensor_scalar(
                z_rows[:, t, cols], h_rows[t][:], moments[:, t, 0:1], factor[:, t : t + 1], ALU.subtract, ALU.mult
            )
        for t, cols in ((3, first_half), (2, second_half), (3, second_half)):
            nc.scalar.activation(
                z_rows[:, t, cols],
                h_banks[t][:, cols],
                ACT.Identity,
                bias=shift[:, t - 2 : t - 1],
                scale=factor[:, t : t + 1],
            )

        z_bf = [sbuf("z_bf%d" % c, [P, CHUNK, PACK], BF16) for c in range(CHUNKS)]

        def weave_z(c, engine_copy):
            weave(engine_copy, z_bf[c][:], z_rows[:, :, c * CHUNK : (c + 1) * CHUNK])

        def second_layer(c, last):
            z_codes = sbuf("z_codes%d" % c, [P, CHUNK], U32)
            z_scales = sbuf("z_scales%d" % c, [P, CHUNK], U8)
            quantize(z_codes[:], z_scales[:], z_bf[c][:].rearrange("p n j -> p (n j)"))
            if last:
                accs = [ps.tile([P, CHUNK], F32, name="acc_last%d" % b, tag="bank%d" % b)[:] for b in range(2)]
            else:
                acc = ps.tile([P, 2, CHUNK], F32, name="acc%d" % c, tag="bank%d" % (PACK + c))
                accs = [acc[:, b, :] for b in range(2)] + [acc[:]]
            for b in range(2):
                cols = slice(b * P, (b + 1) * P)
                nc.tensor.matmul_mx(
                    out=accs[b],
                    lhsT=w2_codes[:, cols].bitcast(FP8X4),
                    lhsT_scale=w2_scales[:, cols],
                    rhs=z_codes[:].bitcast(FP8X4),
                    rhs_scale=z_scales[:],
                    start=True,
                    stop=True,
                )
            return accs

        def store(c, copies):
            res = sbuf("res%d" % c, [P, 2, CHUNK], F32)
            for engine_copy, rows, acc in copies:
                engine_copy(res[:, rows], acc)
            nc.sync.dma_start(out[:, c * CHUNK : (c + 1) * CHUNK].rearrange("(b p) n -> p b n", p=P), res[:])

        weave_z(3, nc.scalar.copy)
        weave_z(0, nc.vector.tensor_copy)
        weave_z(1, nc.vector.tensor_copy)
        acc0 = second_layer(0, False)
        weave_z(2, nc.vector.tensor_copy)
        acc1 = second_layer(1, False)
        acc3 = second_layer(3, False)
        acc2 = second_layer(2, True)
        both = slice(0, 2)
        store(0, [(nc.scalar.copy, both, acc0[2])])
        store(1, [(nc.vector.tensor_copy, both, acc1[2])])
        store(3, [(nc.scalar.copy, both, acc3[2])])
        store(2, [(nc.vector.tensor_copy, 0, acc2[0]), (nc.vector.tensor_copy, 1, acc2[1])])
